import numpy as np
CORES = [0,1]
N = 2
def setup_inputs(rng):
    return {"x": rng.standard_normal((N, 128, 4), dtype=np.float32)}
def reference(x):
    s = x.sum(axis=0, dtype=np.float64).astype(x.dtype)
    return {"y": np.broadcast_to(s, (N,) + s.shape)}

@@ -1,0 +1,27 @@
+from concourse.mybir import AluOpType
+
+SCRATCH = {
+    "mine": ("sbuf", [128, 4], "float32"),
+    "land": ("sbuf", [128, 4], "float32"),
+}
+SEMAPHORES = ["staged", "seeded", "xchg", "stored"]
+
+
+def rank_program(g, core, T, topo):
+    rank = T.rank_of(core)
+    if rank is None:
+        return
+    peer = T.cores[1 - rank]
+    rid, pid, _se = topo.addr(peer)
+
+    g.sync.dma_start(T.mine[:], T.x[:]).then_inc(T.sem.staged, 16)
+    g.scalar.dma_start(T.y[:], T.x[:]).then_inc(T.sem.seeded, 16)
+
+    g.wait_ge(T.sem.staged, 16)
+    g.remote_dma(T.land[:], T.mine[:], remote_sem=T.sem.xchg, local_sem=T.sem.xchg,
+                 pid=pid, routing_id=rid, dma_engine_mask=topo.mask(core, peer))
+
+    g.wait_ge(T.sem.xchg, 32)
+    g.wait_ge(T.sem.seeded, 16)
+    g.dma_start(T.y[:], T.land[:], accum_op=AluOpType.add).then_inc(T.sem.stored, 16)
+    g.wait_ge(T.sem.stored, 16)

@@ -1,10 +1,13 @@
 from concourse.mybir import AluOpType
 
 SCRATCH = {
-    "mine": ("sbuf", [128, 4], "float32"),
-    "land": ("sbuf", [128, 4], "float32"),
+    "mine": ("dram", [128, 4], "float32"),
+    "land": ("dram", [128, 4], "float32"),
 }
 SEMAPHORES = ["staged", "seeded", "xchg", "stored"]
+
+ENGINES = 4
+MASK = (1 << ENGINES) - 1
 
 
 def rank_program(g, core, T, topo):
@@ -19,9 +22,9 @@ def rank_program(g, core, T, topo):
 
     g.wait_ge(T.sem.staged, 16)
     g.remote_dma(T.land[:], T.mine[:], remote_sem=T.sem.xchg, local_sem=T.sem.xchg,
-                 pid=pid, routing_id=rid, dma_engine_mask=topo.mask(core, peer))
+                 pid=pid, routing_id=rid, dma_engine_mask=MASK & topo.mask(core, peer))
 
-    g.wait_ge(T.sem.xchg, 32)
+    g.wait_ge(T.sem.xchg, 2 * ENGINES)
     g.wait_ge(T.sem.seeded, 16)
     g.dma_start(T.y[:], T.land[:], accum_op=AluOpType.add).then_inc(T.sem.stored, 16)
     g.wait_ge(T.sem.stored, 16)

from concourse.mybir import AluOpType

SCRATCH = {
    "mine": ("dram", [128, 4], "float32"),
    "land": ("dram", [128, 4], "float32"),
}
SEMAPHORES = ["staged", "seeded", "xchg", "stored"]

ENGINES = 4
MASK = (1 << ENGINES) - 1


def rank_program(g, core, T, topo):
    rank = T.rank_of(core)
    if rank is None:
        return
    peer = T.cores[1 - rank]
    rid, pid, _se = topo.addr(peer)

    g.sync.dma_start(T.mine[:], T.x[:]).then_inc(T.sem.staged, 16)
    g.scalar.dma_start(T.y[:], T.x[:]).then_inc(T.sem.seeded, 16)

    g.wait_ge(T.sem.staged, 16)
    g.remote_dma(T.land[:], T.mine[:], remote_sem=T.sem.xchg, local_sem=T.sem.xchg,
                 pid=pid, routing_id=rid, dma_engine_mask=MASK & topo.mask(core, peer))

    g.wait_ge(T.sem.xchg, 2 * ENGINES)
    g.wait_ge(T.sem.seeded, 16)
    g.dma_start(T.y[:], T.land[:], accum_op=AluOpType.add).then_inc(T.sem.stored, 16)
    g.wait_ge(T.sem.stored, 16)
